import numpy as np
import ml_dtypes


def mxq(x, axis, fmt="e4m3"):
    dtype, down = {"e4m3": (ml_dtypes.float8_e4m3fn, 7), "e5m2": (ml_dtypes.float8_e5m2, 14)}[fmt]
    v = np.moveaxis(np.asarray(x, np.float32).astype(ml_dtypes.bfloat16).astype(np.float64), axis, -1)
    blocks = v.reshape(v.shape[:-1] + (-1, 32))
    amax = np.abs(blocks).max(-1, keepdims=True)
    byte = np.maximum(np.where(amax > 0, np.frexp(amax)[1] - 1 + 127, 0) - down, 1)
    scale = np.exp2(byte - 127.0)
    codes = (blocks / scale).astype(np.float32).astype(dtype).astype(np.float64)
    return np.moveaxis((codes * scale).reshape(v.shape), -1, axis)


WIDE = False


def mx_kscale(k):
    if not WIDE:
        return np.ones(k)
    levels = np.array([10, -10, 5, -5, 0])
    if k % 512:
        return np.exp2(np.random.permutation(np.resize(levels, k // 32))).repeat(32)
    a = np.empty((k // 512, 16))
    for p in range(k // 512):
        a[p, :8] = np.random.permutation(np.resize(levels, 8))
        for g in range(8):
            far = levels[np.abs(levels - a[p, g]) >= 10]
            a[p, g + 8] = far[np.random.randint(len(far))]
    return np.exp2(a.ravel()).repeat(32)


BF16 = ml_dtypes.bfloat16


def bf(x):
    return np.asarray(x, np.float32).astype(BF16)


def f64(x):
    return np.asarray(x).astype(np.float64)


E2M1 = np.array([0.0, 0.5, 1.0, 1.5, 2.0, 3.0, 4.0, 6.0, -0.0, -0.5, -1.0, -1.5, -2.0, -3.0, -4.0, -6.0])


def pack_weight(w, fmt):
    k, n = w.shape
    w = f64(bf(w)).reshape(k // 32, 32, n)
    amax = np.abs(w).max(1)
    if fmt == "e4m3":
        byte = np.frexp(amax)[1] - 1 + 127 - 7
    else:
        mant, ex = np.frexp(amax / 6.0)
        byte = np.where(mant > 0.5, ex, ex - 1) + 127
    byte = np.clip(np.where(amax > 0, byte, 1), 1, 254)
    scaled = (w * np.exp2(127.0 - byte)[:, None, :]).reshape(k, n).astype(np.float32)
    by_word = np.ascontiguousarray(scaled.reshape(k // 512, 128, 4, n).transpose(0, 1, 3, 2))
    if fmt == "e4m3":
        words = by_word.astype(ml_dtypes.float8_e4m3fn).view(np.uint8)
    else:
        c = by_word.astype(ml_dtypes.float4_e2m1fn).view(np.uint8) & 0xF
        words = c[..., 0::2] | (c[..., 1::2] << 4)
    return np.ascontiguousarray(words), np.ascontiguousarray(byte.astype(np.uint8).reshape(k // 512, 16, n))


def unpack_weight(words, scales, fmt):
    g, p, n, _ = words.shape
    if fmt == "e4m3":
        vals = np.ascontiguousarray(words).view(ml_dtypes.float8_e4m3fn).astype(np.float64)
    else:
        nib = np.empty((g, p, n, 4), np.uint8)
        nib[..., 0::2] = words & 0xF
        nib[..., 1::2] = words >> 4
        vals = E2M1[nib]
    vals = vals * np.repeat(np.exp2(scales.astype(np.float64) - 127.0), 8, axis=1)[..., None]
    return vals.transpose(0, 1, 3, 2).reshape(g * 512, n)
def pack4(w):
    words, scales = pack_weight(w, "e2m1")
    return words.reshape(words.shape[0], 128, -1), scales


def unpack4(words, scales):
    return unpack_weight(words.reshape(words.shape[0], 128, -1, 2), scales, "e2m1")


S, R, T, B, C, Q = 8, 512, 512, 8, 64, 512


def setup_inputs():
    s, t = mx_kscale(R), mx_kscale(T)
    v = mx_kscale(Q)[::C]
    m = v[:, None] * s
    j = m.reshape(S, B, C).transpose(1, 0, 2).reshape(B, Q)
    x = np.random.standard_normal((S, R, T)) * m[:, :, None] * t
    a = 0.35 * np.random.standard_normal((R, R)) / np.sqrt(R) / s[:, None] * s
    f = 0.35 * np.random.standard_normal((T, T)) / np.sqrt(T) / t[:, None] * t
    d = 0.35 * np.random.standard_normal((B, Q, Q)) / np.sqrt(Q) / j[:, :, None] * j[:, None, :]
    a_words, a_scales = pack4(a)
    f_words, f_scales = pack4(f)
    d_words, d_scales = pack4(d.reshape(B * Q, Q))
    return {"x": bf(x),
            "a_words": a_words, "a_scales": a_scales,
            "f_words": f_words, "f_scales": f_scales,
            "d_words": d_words, "d_scales": d_scales,
            "trace": bf((1 + 0.1 * np.random.standard_normal((S, R))) / m),
            "gain": bf((1 + 0.1 * np.random.standard_normal(T)) / t)}


def reference(x, a_words, a_scales, f_words, f_scales, d_words, d_scales, trace, gain):
    x = f64(x)
    a = unpack4(a_words, a_scales)
    f = unpack4(f_words, f_scales)
    d = unpack4(d_words, d_scales).reshape(B, Q, Q)
    h = x + (a.T @ mxq(x, 1, "e4m3"))
    y = h + (mxq(h, 2, "e4m3") @ f)
    y = y.reshape(S, B, C, T).transpose(1, 0, 2, 3).reshape(B, Q, T)
    z = y + (d.swapaxes(1, 2) @ mxq(y, 1, "e4m3"))
    z = z.reshape(B, S, C, T).transpose(1, 0, 2, 3).reshape(S, R, T)
    return z * f64(trace)[:, :, None] * f64(gain)

@@ -1,0 +1,377 @@
+from contextlib import ExitStack
+
+import concourse.mybir as mybir
+from concourse.masks import make_identity
+
+S, R, T, B, C, Q = 8, 512, 512, 8, 64, 512
+FLOPS = 3 * 2 * S * R * T * 512
+
+F32 = mybir.dt.float32
+BF16 = mybir.dt.bfloat16
+I32 = mybir.dt.int32
+U32 = mybir.dt.uint32
+U8 = mybir.dt.uint8
+FP8X4 = mybir.dt.float8_e4m3fn_x4
+FP4X4 = mybir.dt.float4_e2m1fn_x4
+ALU = mybir.AluOpType
+ACT = mybir.ActivationFunctionType
+
+P = 128
+NB = 4
+XI_ENGINE = "VSGSSGSS"
+
+
+def tile_seismic_gather_coupling_t2_kernel(
+    tc, x, a_words, a_scales, f_words, f_scales, d_words, d_scales, trace, gain, out
+):
+    nc = tc.nc
+    with ExitStack() as ctx:
+        pool = ctx.enter_context(tc.tile_pool(name="sb", bufs=1))
+        psum = ctx.enter_context(tc.psum_pool(name="ps", bufs=4))
+        ctx.enter_context(tc.manual_schedule())
+
+        def sb(shape, dt, name, bufs=1, tag=None):
+            return pool.tile(shape, dt, name=name, tag=tag or name, bufs=bufs, align_bytes=64)
+
+        def bank(shape, kind, name):
+            return psum.tile(shape, F32, name=name, tag=kind)
+
+        ident = sb([P, P], F32, "ident")
+        make_identity(nc, ident[:])
+        af_scales = sb([P, 2, 512], U8, "af_scales")
+        nc.vector.memset(af_scales[:].bitcast(I32), 0)
+        d_sc = sb([P, B, 512], U8, "d_sc")
+        trace_rows = sb([P, P], BF16, "trace_rows")
+        nc.vector.memset(trace_rows[:], 0.0)
+        nc.vector.memset(d_sc[:].bitcast(I32), 0)
+
+        gain_bf = sb([P, 4], BF16, "gain_bf")
+        nc.scalar.dma_start(out=gain_bf[:], in_=gain.rearrange("(m t) -> m t", t=4))
+        for which, src in ((0, a_scales), (1, f_scales)):
+            for q in range(4):
+                nc.scalar.dma_start(
+                    out=af_scales[32 * q : 32 * q + 4, which, :].bitcast(I32),
+                    in_=src[0, 4 * q : 4 * q + 4, :].bitcast(I32),
+                )
+        nc.scalar.dma_start(
+            out=trace_rows[0:32, :], in_=trace.rearrange("i (g p) -> (i g) p", p=P)
+        )
+        gain_f = sb([P, 4], F32, "gain_f")
+        nc.scalar.copy(out=gain_f[:], in_=gain_bf[:])
+
+        raw = []
+        for k in range(4):
+            pair = sb([P, 2, 4, T], BF16, f"raw{k}", bufs=4, tag="wide")
+            raw.append(pair)
+        a_w = sb([P, 1024], U8, "a_w")
+        f_w = sb([P, 1024], U8, "f_w")
+        d_w = sb([P, B, 1024], U8, "d_w")
+
+        def load_x(i):
+            nc.sync.dma_start(
+                out=raw[i // 2][:, i % 2], in_=x[i].rearrange("(p j) e -> p j e", j=4)
+            )
+
+        load_x(0)
+        nc.sync.dma_start(out=a_w[:].bitcast(I32), in_=a_words[0].bitcast(I32))
+        for i in range(1, S):
+            load_x(i)
+        nc.sync.dma_start(out=f_w[:].bitcast(I32), in_=f_words[0].bitcast(I32))
+        nc.sync.dma_start(
+            out=d_w[:].bitcast(I32), in_=d_words.bitcast(I32).rearrange("b p n -> p b n")
+        )
+        for q in range(4):
+            nc.sync.dma_start(
+                out=d_sc[32 * q : 32 * q + 4, :, :].bitcast(I32),
+                in_=d_scales[:, 4 * q : 4 * q + 4, :].bitcast(I32).rearrange("b q n -> q b n"),
+            )
+
+        xb, xt, xq = {}, {}, {}
+
+        def interleave_x(i):
+            xb[i] = sb([P, 512, 4], BF16, f"xb{i}", bufs=3, tag="pre")
+            dst = xb[i][:].rearrange("p (t m) j -> p t m j", t=4)
+            src = raw[i // 2][:, i % 2].rearrange("p j (m t) -> p t m j", t=4)
+            if XI_ENGINE[i] == "V":
+                nc.vector.tensor_copy(out=dst, in_=src)
+            elif XI_ENGINE[i] == "S":
+                nc.scalar.copy(out=dst, in_=src)
+            else:
+                nc.gpsimd.tensor_scalar(
+                    out=dst, in0=src, scalar1=1.0, scalar2=0.0, op0=ALU.mult, op1=ALU.add
+                )
+
+        def transpose_x(i):
+            xt[i] = sb([P, R, 4], BF16, f"xt{i}", bufs=8, tag="four")
+            words = raw[i // 2][:].rearrange("p s j e -> p (s j e)").bitcast(F32)
+            dst = xt[i][:].rearrange("p r t -> p (r t)").bitcast(F32)
+            dst = dst.rearrange("p (r j u) -> p r j u", j=4, u=2)
+            banks = []
+            for k in range(2):
+                ps = bank([P, 2, 2, P], "tr", f"xps{i}_{k}")
+                for jj in range(2):
+                    base = ((i % 2) * 4 + 2 * k + jj) * 256
+                    for u in range(2):
+                        nc.tensor.transpose(
+                            ps[:, jj, u, :], words[:, base + u : base + 256 : 2], ident[:]
+                        )
+                banks.append(ps)
+            for k in range(2):
+                nc.scalar.copy(
+                    out=dst[:, :, 2 * k : 2 * k + 2, :],
+                    in_=banks[k][:].rearrange("p j u r -> p r j u"),
+                )
+
+        def quantize(src, width, name, tag, bufs):
+            codes = sb([P, width], U32, name + "c", bufs=bufs, tag=tag + "c")
+            scales = sb([P, width], U8, name + "s", bufs=bufs, tag=tag + "s")
+            nc.vector.quantize_mx(out=codes[:].bitcast(FP8X4), scales=scales[:], in_=src)
+            return codes, scales
+
+        def quantize_x(i):
+            xq[i] = quantize(xb[i][:].rearrange("p c j -> p (c j)"), 512, f"xq{i}", "xq", 8)
+
+        h = []
+        for g in range(NB):
+            hg = sb([P, 2, S, C, 4], F32, f"h{g}", bufs=5, tag="big")
+            h.append(hg)
+
+        def stage1(i, g):
+            ps = bank([P, 4, P], "mx", f"hps{i}_{g}")
+            codes, scales = xq[i]
+            cols = slice(P * g, P * g + P)
+            for t in range(4):
+                tc_ = slice(P * t, P * t + P)
+                nc.tensor.matmul_mx(
+                    out=ps[:, t, :],
+                    lhsT=codes[:, tc_].bitcast(FP8X4),
+                    lhsT_scale=scales[:, tc_],
+                    rhs=a_w[:, 256 * g : 256 * g + 256].bitcast(FP4X4),
+                    rhs_scale=af_scales[:, 0, cols],
+                    start=True,
+                    stop=True,
+                )
+            nc.vector.tensor_tensor(
+                out=h[g][:, :, i, :, :],
+                in0=ps[:].rearrange("p t (b c) -> p b c t", b=2),
+                in1=xt[i][:, cols, :].rearrange("p (b c) t -> p b c t", b=2),
+                op=ALU.add,
+            )
+
+        LA = 2
+        for i in range(LA):
+            interleave_x(i)
+            transpose_x(i)
+        for i in range(S):
+            quantize_x(i)
+            if i + LA < S:
+                interleave_x(i + LA)
+                transpose_x(i + LA)
+            if i >= 1:
+                for g in range(NB):
+                    stage1(i - 1, g)
+        for g in range(NB):
+            stage1(S - 1, g)
+
+        f_p = sb([P, 1024], U8, "f_p")
+        nc.gpsimd.tensor_copy(
+            out=f_p[:].rearrange("p (t m k) -> p t m k", t=4, k=2),
+            in_=f_w[:].rearrange("p (m t k) -> p t m k", t=4, k=2),
+        )
+        f_sc = sb([P, 512], U8, "f_sc")
+        nc.gpsimd.tensor_copy(
+            out=f_sc[:].rearrange("p (t m) -> p t m", t=4),
+            in_=af_scales[:, 1, :].rearrange("p (m t) -> p t m", t=4),
+        )
+
+        trace_f = sb([P, P], F32, "trace_f")
+        nc.vector.tensor_copy(out=trace_f[:], in_=trace_rows[:])
+        tps = bank([P, P], "tr", "tps")
+        nc.tensor.transpose(tps[:], trace_f[:], ident[:])
+        trace_c = sb([P, 32], F32, "trace_c")
+        nc.scalar.copy(out=trace_c[:], in_=tps[:, 0:32])
+
+        hb, hq, yt, yb, yqc, yqs, rr, zt = {}, {}, {}, {}, {}, {}, {}, {}
+        fps, dps, yps = {}, {}, {}
+
+        def hband(b):
+            return h[b // 2][:, b % 2]
+
+        def cast(b, half):
+            if half == 0:
+                hb[b] = sb([P, 2048], BF16, f"hb{b}", bufs=3, tag="pre")
+            nc.scalar.copy(
+                out=hb[b][:, 1024 * half : 1024 * half + 1024],
+                in_=hband(b)[:, 4 * half : 4 * half + 4].rearrange("p i c t -> p (i c t)"),
+            )
+
+        def residual(b):
+            rr[b] = sb([P, 4, 512], F32, f"rr{b}", bufs=4, tag="wide")
+            src = hband(b).rearrange("p i c t -> p t (i c)")
+            for t in range(4):
+                nc.gpsimd.tensor_scalar(
+                    out=rr[b][:, t, :],
+                    in0=src[:, t, :],
+                    scalar1=gain_f[:, t : t + 1],
+                    scalar2=0.0,
+                    op0=ALU.mult,
+                    op1=ALU.add,
+                )
+
+        def quantize_h(b):
+            hq[b] = quantize(hb[b][:], 512, f"hq{b}", "hq", 3)
+
+        def f_pass(ps, b, t, stop):
+            codes, scales = hq[b]
+            nc.tensor.matmul_mx(
+                out=ps[:],
+                lhsT=f_p[:, 256 * t : 256 * t + 256].bitcast(FP4X4),
+                lhsT_scale=f_sc[:, P * t : P * t + P],
+                rhs=codes[:].bitcast(FP8X4),
+                rhs_scale=scales[:],
+                start=True,
+                stop=stop,
+            )
+
+        def stage2(b, ts):
+            for t in ts:
+                fps[b, t] = bank([P, 512], "mx", f"fps{b}_{t}")
+                f_pass(fps[b, t], b, t, True)
+
+        def add_y(b, ts):
+            if ts[0] == 0:
+                yt[b] = sb([P, 4, 512], BF16, f"yt{b}", bufs=8, tag="four")
+            src = hband(b).rearrange("p i (k u e) t -> p t u (i k) e", u=2, e=2)
+            for t in ts:
+                nc.vector.tensor_tensor(
+                    out=yt[b][:, t, :].rearrange("p (u x e) -> p u x e", u=2, e=2),
+                    in0=fps[b, t][:].rearrange("p (x u e) -> p u x e", u=2, e=2),
+                    in1=src[:, t],
+                    op=ALU.add,
+                )
+
+        def transpose_y(b, half):
+            words = yt[b][:].rearrange("p t c -> p (t c)").bitcast(F32)
+            ps = bank([P, 2, 2, P], "tr", f"yps{b}_{half}")
+            for tt in range(2):
+                for u in range(2):
+                    base = (2 * half + tt) * 256 + u * P
+                    nc.tensor.transpose(ps[:, tt, u, :], words[:, base : base + P], ident[:])
+            yps[b, half] = ps
+
+        def copy_y(b, half):
+            if half == 0:
+                yb[b] = sb([P, 2048], BF16, f"yb{b}", bufs=8, tag="four")
+            dst = yb[b][:].bitcast(F32).rearrange("p (t m u) -> p t m u", t=4, u=2)
+            nc.scalar.copy(
+                out=dst[:, 2 * half : 2 * half + 2],
+                in_=yps[b, half][:].rearrange("p t u m -> p t m u"),
+            )
+
+        def quantize_y(b, half):
+            if half == 0:
+                yqc[b] = sb([P, 512], U32, f"yqc{b}", bufs=2, tag="yqc")
+                yqs[b] = sb([P, 512], U8, f"yqs{b}", bufs=2, tag="yqs")
+            cols = slice(256 * half, 256 * half + 256)
+            nc.vector.quantize_mx(
+                out=yqc[b][:, cols].bitcast(FP8X4),
+                scales=yqs[b][:, cols],
+                in_=yb[b][:, 1024 * half : 1024 * half + 1024],
+            )
+
+        def stage3(b, ts):
+            for t in ts:
+                ps = bank([P, 512], "mx", f"dps{b}_{t}")
+                f_pass(ps, b, t, False)
+                tc_ = slice(P * t, P * t + P)
+                nc.tensor.matmul_mx(
+                    out=ps[:],
+                    lhsT=yqc[b][:, tc_].bitcast(FP8X4),
+                    lhsT_scale=yqs[b][:, tc_],
+                    rhs=d_w[:, b, :].bitcast(FP4X4),
+                    rhs_scale=d_sc[:, b, :],
+                    start=False,
+                    stop=True,
+                )
+                dps[b, t] = ps
+
+        def add_z(b, ts):
+            g = b // 2
+            if b % 2 == 0 and ts[0] == 0:
+                zt[g] = sb([P, 4, S, 2, C], F32, f"zt{g}", bufs=5, tag="big")
+            for t in ts:
+                nc.vector.scalar_tensor_tensor(
+                    out=zt[g][:, t, :, b % 2, :],
+                    in0=dps[b, t][:].rearrange("p (i c) -> p i c", c=C),
+                    scalar=gain_f[:, t : t + 1],
+                    in1=rr[b][:, t, :].rearrange("p (i c) -> p i c", c=C),
+                    op0=ALU.mult,
+                    op1=ALU.add,
+                )
+
+        def finish(g, sources, share):
+            banks = {}
+            for i in sources:
+                ps = bank([P, 4, P], "tr", f"zps{g}_{i}")
+                for t in range(4):
+                    nc.tensor.transpose(
+                        ps[:, t, :], zt[g][:, t, i].rearrange("p b c -> p (b c)"), ident[:]
+                    )
+                banks[i] = ps
+            for i in sources:
+                o = sb([P, T], F32, f"o{g}_{i}", bufs=6, tag="o")
+                dst = o[:].rearrange("p (m t) -> p m t", t=4)
+                src = banks[i][:].rearrange("p t m -> p m t")
+                tr = trace_c[:, 4 * i + g : 4 * i + g + 1]
+                if share and i % 2 == 1:
+                    nc.vector.tensor_scalar_mul(out=dst, in0=src, scalar1=tr)
+                else:
+                    nc.scalar.activation(out=dst, in_=src, func=ACT.Copy, scale=tr)
+                nc.sync.dma_start(out=out[i, P * g : P * g + P, :], in_=o[:])
+
+        FIRST, SECOND = (0, 1), (2, 3)
+        cast(0, 0)
+        cast(0, 1)
+        residual(0)
+        quantize_h(0)
+        cast(1, 0)
+        cast(1, 1)
+        stage2(0, (0, 1, 2, 3))
+        for k in range(B + 1):
+            if k < B:
+                add_y(k, FIRST)
+                transpose_y(k, 0)
+            if k >= 1:
+                stage3(k - 1, FIRST)
+            if k < B:
+                copy_y(k, 0)
+                add_y(k, SECOND)
+                transpose_y(k, 1)
+            if k >= 1:
+                stage3(k - 1, SECOND)
+            if k < B:
+                copy_y(k, 1)
+            if k + 1 < B:
+                residual(k + 1)
+            if k + 2 < B:
+                cast(k + 2, 0)
+            if k + 1 < B:
+                quantize_h(k + 1)
+            if k >= 1:
+                add_z(k - 1, FIRST)
+            if k + 1 < B:
+                stage2(k + 1, FIRST)
+            if k < B:
+                quantize_y(k, 0)
+            if k + 2 < B:
+                cast(k + 2, 1)
+            if k >= 1:
+                add_z(k - 1, SECOND)
+            if k + 1 < B:
+                stage2(k + 1, SECOND)
+            if k < B:
+                quantize_y(k, 1)
+            if k >= 2:
+                last = k == B
+                finish((k - 2) // 2, range(0, 4) if k % 2 == 0 else range(4, 8), last)
+        finish(NB - 1, range(4, 8), True)

@@ -133,7 +133,7 @@ def tile_seismic_gather_coupling_t2_kernel(
 
         h = []
         for g in range(NB):
-            hg = sb([P, 2, S, C, 4], F32, f"h{g}", bufs=5, tag="big")
+            hg = sb([P, 2, 2, S, C, 2], F32, f"h{g}", bufs=5, tag="big")
             h.append(hg)
 
         def stage1(i, g):
@@ -152,9 +152,9 @@ def tile_seismic_gather_coupling_t2_kernel(
                     stop=True,
                 )
             nc.vector.tensor_tensor(
-                out=h[g][:, :, i, :, :],
-                in0=ps[:].rearrange("p t (b c) -> p b c t", b=2),
-                in1=xt[i][:, cols, :].rearrange("p (b c) t -> p b c t", b=2),
+                out=h[g][:, :, :, i],
+                in0=ps[:].rearrange("p (u e) (b c) -> p u b c e", u=2, b=2),
+                in1=xt[i][:, cols, :].rearrange("p (b c) (u e) -> p u b c e", u=2, b=2),
                 op=ALU.add,
             )
 
@@ -195,23 +195,23 @@ def tile_seismic_gather_coupling_t2_kernel(
         fps, dps, yps = {}, {}, {}
 
         def hband(b):
-            return h[b // 2][:, b % 2]
+            return h[b // 2][:, :, b % 2]
 
         def cast(b, half):
             if half == 0:
                 hb[b] = sb([P, 2048], BF16, f"hb{b}", bufs=3, tag="pre")
             nc.scalar.copy(
-                out=hb[b][:, 1024 * half : 1024 * half + 1024],
-                in_=hband(b)[:, 4 * half : 4 * half + 4].rearrange("p i c t -> p (i c t)"),
+                out=hb[b][:, 1024 * half : 1024 * half + 1024].rearrange("p (n u e) -> p n u e", u=2, e=2),
+                in_=hband(b)[:, :, 4 * half : 4 * half + 4].rearrange("p u i c e -> p (i c) u e"),
             )
 
         def residual(b):
             rr[b] = sb([P, 4, 512], F32, f"rr{b}", bufs=4, tag="wide")
-            src = hband(b).rearrange("p i c t -> p t (i c)")
+            src = hband(b).rearrange("p u i c e -> p u e (i c)")
             for t in range(4):
                 nc.gpsimd.tensor_scalar(
                     out=rr[b][:, t, :],
-                    in0=src[:, t, :],
+                    in0=src[:, t // 2, t % 2],
                     scalar1=gain_f[:, t : t + 1],
                     scalar2=0.0,
                     op0=ALU.mult,
@@ -241,12 +241,12 @@ def tile_seismic_gather_coupling_t2_kernel(
         def add_y(b, ts):
             if ts[0] == 0:
                 yt[b] = sb([P, 4, 512], BF16, f"yt{b}", bufs=8, tag="four")
-            src = hband(b).rearrange("p i (k u e) t -> p t u (i k) e", u=2, e=2)
+            src = hband(b).rearrange("p v i (k u e) w -> p v w u (i k) e", u=2, e=2)
             for t in ts:
                 nc.vector.tensor_tensor(
                     out=yt[b][:, t, :].rearrange("p (u x e) -> p u x e", u=2, e=2),
                     in0=fps[b, t][:].rearrange("p (x u e) -> p u x e", u=2, e=2),
-                    in1=src[:, t],
+                    in1=src[:, t // 2, t % 2],
                     op=ALU.add,
                 )
 

@@ -18,7 +18,7 @@ ACT = mybir.ActivationFunctionType
 
 P = 128
 NB = 4
-XI_ENGINE = "VSGSSGSS"
+XI_ENGINE = "**GSSGSS"
 
 
 def tile_seismic_gather_coupling_t2_kernel(
@@ -86,14 +86,23 @@ def tile_seismic_gather_coupling_t2_kernel(
                 in_=d_scales[:, 4 * q : 4 * q + 4, :].bitcast(I32).rearrange("b q n -> q b n"),
             )
 
-        xb, xt, xq = {}, {}, {}
+        xb, xt, xq, xps = {}, {}, {}, {}
 
         def interleave_x(i):
             xb[i] = sb([P, 512, 4], BF16, f"xb{i}", bufs=3, tag="pre")
             dst = xb[i][:].rearrange("p (t m) j -> p t m j", t=4)
             src = raw[i // 2][:, i % 2].rearrange("p j (m t) -> p t m j", t=4)
-            if XI_ENGINE[i] == "V":
-                nc.vector.tensor_copy(out=dst, in_=src)
+            if XI_ENGINE[i] == "*":
+                nc.vector.tensor_copy(out=dst[:, 0:2], in_=src[:, 0:2])
+                nc.scalar.copy(out=dst[:, 2], in_=src[:, 2])
+                nc.gpsimd.tensor_scalar(
+                    out=dst[:, 3],
+                    in0=src[:, 3],
+                    scalar1=1.0,
+                    scalar2=0.0,
+                    op0=ALU.mult,
+                    op1=ALU.add,
+                )
             elif XI_ENGINE[i] == "S":
                 nc.scalar.copy(out=dst, in_=src)
             else:
@@ -102,11 +111,7 @@ def tile_seismic_gather_coupling_t2_kernel(
                 )
 
         def transpose_x(i):
-            xt[i] = sb([P, R, 4], BF16, f"xt{i}", bufs=8, tag="four")
             words = raw[i // 2][:].rearrange("p s j e -> p (s j e)").bitcast(F32)
-            dst = xt[i][:].rearrange("p r t -> p (r t)").bitcast(F32)
-            dst = dst.rearrange("p (r j u) -> p r j u", j=4, u=2)
-            banks = []
             for k in range(2):
                 ps = bank([P, 2, 2, P], "tr", f"xps{i}_{k}")
                 for jj in range(2):
@@ -115,11 +120,16 @@ def tile_seismic_gather_coupling_t2_kernel(
                         nc.tensor.transpose(
                             ps[:, jj, u, :], words[:, base + u : base + 256 : 2], ident[:]
                         )
-                banks.append(ps)
+                xps[i, k] = ps
+
+        def copy_xt(i):
+            xt[i] = sb([P, R, 4], BF16, f"xt{i}", bufs=8, tag="four")
+            dst = xt[i][:].rearrange("p r t -> p (r t)").bitcast(F32)
+            dst = dst.rearrange("p (r j u) -> p r j u", j=4, u=2)
             for k in range(2):
                 nc.scalar.copy(
                     out=dst[:, :, 2 * k : 2 * k + 2, :],
-                    in_=banks[k][:].rearrange("p j u r -> p r j u"),
+                    in_=xps[i, k][:].rearrange("p j u r -> p r j u"),
                 )
 
         def quantize(src, width, name, tag, bufs):
@@ -136,8 +146,11 @@ def tile_seismic_gather_coupling_t2_kernel(
             hg = sb([P, 2, 2, S, C, 2], F32, f"h{g}", bufs=5, tag="big")
             h.append(hg)
 
+        hps = {}
+
         def stage1(i, g):
             ps = bank([P, 4, P], "mx", f"hps{i}_{g}")
+            hps[i, g] = ps
             codes, scales = xq[i]
             cols = slice(P * g, P * g + P)
             for t in range(4):
@@ -151,6 +164,10 @@ def tile_seismic_gather_coupling_t2_kernel(
                     start=True,
                     stop=True,
                 )
+
+        def add_h(i, g):
+            ps = hps[i, g]
+            cols = slice(P * g, P * g + P)
             nc.vector.tensor_tensor(
                 out=h[g][:, :, :, i],
                 in0=ps[:].rearrange("p (u e) (b c) -> p u b c e", u=2, b=2),
@@ -158,20 +175,29 @@ def tile_seismic_gather_coupling_t2_kernel(
                 op=ALU.add,
             )
 
-        LA = 2
-        for i in range(LA):
+        for i in range(2):
             interleave_x(i)
             transpose_x(i)
-        for i in range(S):
+            copy_xt(i)
             quantize_x(i)
-            if i + LA < S:
-                interleave_x(i + LA)
-                transpose_x(i + LA)
-            if i >= 1:
-                for g in range(NB):
-                    stage1(i - 1, g)
-        for g in range(NB):
-            stage1(S - 1, g)
+        interleave_x(2)
+        interleave_x(3)
+        for i in range(S):
+            stage1(i, 0)
+            stage1(i, 1)
+            if i + 2 < S:
+                quantize_x(i + 2)
+            add_h(i, 0)
+            stage1(i, 2)
+            add_h(i, 1)
+            stage1(i, 3)
+            add_h(i, 2)
+            add_h(i, 3)
+            if i + 4 < S:
+                interleave_x(i + 4)
+            if i + 2 < S:
+                transpose_x(i + 2)
+                copy_xt(i + 2)
 
         f_p = sb([P, 1024], U8, "f_p")
         nc.gpsimd.tensor_copy(
@@ -191,7 +217,7 @@ def tile_seismic_gather_coupling_t2_kernel(
         trace_c = sb([P, 32], F32, "trace_c")
         nc.scalar.copy(out=trace_c[:], in_=tps[:, 0:32])
 
-        hb, hq, yt, yb, yqc, yqs, rr, zt = {}, {}, {}, {}, {}, {}, {}, {}
+        hb, hq, yt, yb, yq, rr, zt = {}, {}, {}, {}, {}, {}, {}
         fps, dps, yps = {}, {}, {}
 
         def hband(b):
@@ -268,26 +294,19 @@ def tile_seismic_gather_coupling_t2_kernel(
                 in_=yps[b, half][:].rearrange("p t u m -> p t m u"),
             )
 
-        def quantize_y(b, half):
-            if half == 0:
-                yqc[b] = sb([P, 512], U32, f"yqc{b}", bufs=2, tag="yqc")
-                yqs[b] = sb([P, 512], U8, f"yqs{b}", bufs=2, tag="yqs")
-            cols = slice(256 * half, 256 * half + 256)
-            nc.vector.quantize_mx(
-                out=yqc[b][:, cols].bitcast(FP8X4),
-                scales=yqs[b][:, cols],
-                in_=yb[b][:, 1024 * half : 1024 * half + 1024],
-            )
+        def quantize_y(b):
+            yq[b] = quantize(yb[b][:], 512, f"yq{b}", "yq", 2)
 
         def stage3(b, ts):
             for t in ts:
                 ps = bank([P, 512], "mx", f"dps{b}_{t}")
                 f_pass(ps, b, t, False)
                 tc_ = slice(P * t, P * t + P)
+                codes, scales = yq[b]
                 nc.tensor.matmul_mx(
                     out=ps[:],
-                    lhsT=yqc[b][:, tc_].bitcast(FP8X4),
-                    lhsT_scale=yqs[b][:, tc_],
+                    lhsT=codes[:, tc_].bitcast(FP8X4),
+                    lhsT_scale=scales[:, tc_],
                     rhs=d_w[:, b, :].bitcast(FP4X4),
                     rhs_scale=d_sc[:, b, :],
                     start=False,
@@ -295,21 +314,22 @@ def tile_seismic_gather_coupling_t2_kernel(
                 )
                 dps[b, t] = ps
 
-        def add_z(b, ts):
+        def add_z(b, ts, sources=(0, S)):
             g = b // 2
+            i0, i1 = sources
             if b % 2 == 0 and ts[0] == 0:
                 zt[g] = sb([P, 4, S, 2, C], F32, f"zt{g}", bufs=5, tag="big")
             for t in ts:
                 nc.vector.scalar_tensor_tensor(
-                    out=zt[g][:, t, :, b % 2, :],
-                    in0=dps[b, t][:].rearrange("p (i c) -> p i c", c=C),
+                    out=zt[g][:, t, i0:i1, b % 2, :],
+                    in0=dps[b, t][:, C * i0 : C * i1].rearrange("p (i c) -> p i c", c=C),
                     scalar=gain_f[:, t : t + 1],
-                    in1=rr[b][:, t, :].rearrange("p (i c) -> p i c", c=C),
+                    in1=rr[b][:, t, C * i0 : C * i1].rearrange("p (i c) -> p i c", c=C),
                     op0=ALU.mult,
                     op1=ALU.add,
                 )
 
-        def finish(g, sources, share):
+        def finish_z(g, sources, share):
             banks = {}
             for i in sources:
                 ps = bank([P, 4, P], "tr", f"zps{g}_{i}")
@@ -330,48 +350,50 @@ def tile_seismic_gather_coupling_t2_kernel(
                 nc.sync.dma_start(out=out[i, P * g : P * g + P, :], in_=o[:])
 
         FIRST, SECOND = (0, 1), (2, 3)
-        cast(0, 0)
-        cast(0, 1)
+
+        def finish_step(k, part):
+            if k >= 2:
+                first = 4 * (k % 2)
+                part((k - 2) // 2, range(first, first + 4), k >= B)
+
+        for b in (0, 1):
+            cast(b, 0)
+            cast(b, 1)
         residual(0)
+        residual(1)
         quantize_h(0)
-        cast(1, 0)
-        cast(1, 1)
-        stage2(0, (0, 1, 2, 3))
-        for k in range(B + 1):
+        stage2(0, FIRST)
+        stage2(0, SECOND)
+        for k in range(B + 2):
             if k < B:
                 add_y(k, FIRST)
-                transpose_y(k, 0)
-            if k >= 1:
+            if 1 <= k <= B:
                 stage3(k - 1, FIRST)
             if k < B:
-                copy_y(k, 0)
                 add_y(k, SECOND)
+                transpose_y(k, 0)
                 transpose_y(k, 1)
-            if k >= 1:
-                stage3(k - 1, SECOND)
-            if k < B:
+                copy_y(k, 0)
                 copy_y(k, 1)
+            if 1 <= k <= B:
+                add_z(k - 1, FIRST, (0, S if k < B else 4))
+                stage3(k - 1, SECOND)
             if k + 1 < B:
-                residual(k + 1)
+                quantize_h(k + 1)
+                stage2(k + 1, FIRST)
             if k + 2 < B:
                 cast(k + 2, 0)
             if k + 1 < B:
-                quantize_h(k + 1)
-            if k >= 1:
-                add_z(k - 1, FIRST)
-            if k + 1 < B:
-                stage2(k + 1, FIRST)
+                stage2(k + 1, SECOND)
+            if 1 <= k <= B:
+                add_z(k - 1, SECOND, (0, S if k < B else 4))
+            if k == B:
+                add_z(k - 1, FIRST, (4, S))
+                add_z(k - 1, SECOND, (4, S))
             if k < B:
-                quantize_y(k, 0)
+                quantize_y(k)
+            if k + 2 < B:
+                residual(k + 2)
+            finish_step(k, finish_z)
             if k + 2 < B:
                 cast(k + 2, 1)
-            if k >= 1:
-                add_z(k - 1, SECOND)
-            if k + 1 < B:
-                stage2(k + 1, SECOND)
-            if k < B:
-                quantize_y(k, 1)
-            if k >= 2:
-                last = k == B
-                finish((k - 2) // 2, range(0, 4) if k % 2 == 0 else range(4, 8), last)
-        finish(NB - 1, range(4, 8), True)

from contextlib import ExitStack

import concourse.mybir as mybir
from concourse.masks import make_identity

S, R, T, B, C, Q = 8, 512, 512, 8, 64, 512
FLOPS = 3 * 2 * S * R * T * 512

F32 = mybir.dt.float32
BF16 = mybir.dt.bfloat16
I32 = mybir.dt.int32
U32 = mybir.dt.uint32
U8 = mybir.dt.uint8
FP8X4 = mybir.dt.float8_e4m3fn_x4
FP4X4 = mybir.dt.float4_e2m1fn_x4
ALU = mybir.AluOpType
ACT = mybir.ActivationFunctionType

P = 128
NB = 4
XI_ENGINE = "**GSSGSS"


def tile_seismic_gather_coupling_t2_kernel(
    tc, x, a_words, a_scales, f_words, f_scales, d_words, d_scales, trace, gain, out
):
    nc = tc.nc
    with ExitStack() as ctx:
        pool = ctx.enter_context(tc.tile_pool(name="sb", bufs=1))
        psum = ctx.enter_context(tc.psum_pool(name="ps", bufs=4))
        ctx.enter_context(tc.manual_schedule())

        def sb(shape, dt, name, bufs=1, tag=None):
            return pool.tile(shape, dt, name=name, tag=tag or name, bufs=bufs, align_bytes=64)

        def bank(shape, kind, name):
            return psum.tile(shape, F32, name=name, tag=kind)

        ident = sb([P, P], F32, "ident")
        make_identity(nc, ident[:])
        af_scales = sb([P, 2, 512], U8, "af_scales")
        nc.vector.memset(af_scales[:].bitcast(I32), 0)
        d_sc = sb([P, B, 512], U8, "d_sc")
        trace_rows = sb([P, P], BF16, "trace_rows")
        nc.vector.memset(trace_rows[:], 0.0)
        nc.vector.memset(d_sc[:].bitcast(I32), 0)

        gain_bf = sb([P, 4], BF16, "gain_bf")
        nc.scalar.dma_start(out=gain_bf[:], in_=gain.rearrange("(m t) -> m t", t=4))
        for which, src in ((0, a_scales), (1, f_scales)):
            for q in range(4):
                nc.scalar.dma_start(
                    out=af_scales[32 * q : 32 * q + 4, which, :].bitcast(I32),
                    in_=src[0, 4 * q : 4 * q + 4, :].bitcast(I32),
                )
        nc.scalar.dma_start(
            out=trace_rows[0:32, :], in_=trace.rearrange("i (g p) -> (i g) p", p=P)
        )
        gain_f = sb([P, 4], F32, "gain_f")
        nc.scalar.copy(out=gain_f[:], in_=gain_bf[:])

        raw = []
        for k in range(4):
            pair = sb([P, 2, 4, T], BF16, f"raw{k}", bufs=4, tag="wide")
            raw.append(pair)
        a_w = sb([P, 1024], U8, "a_w")
        f_w = sb([P, 1024], U8, "f_w")
        d_w = sb([P, B, 1024], U8, "d_w")

        def load_x(i):
            nc.sync.dma_start(
                out=raw[i // 2][:, i % 2], in_=x[i].rearrange("(p j) e -> p j e", j=4)
            )

        load_x(0)
        nc.sync.dma_start(out=a_w[:].bitcast(I32), in_=a_words[0].bitcast(I32))
        for i in range(1, S):
            load_x(i)
        nc.sync.dma_start(out=f_w[:].bitcast(I32), in_=f_words[0].bitcast(I32))
        nc.sync.dma_start(
            out=d_w[:].bitcast(I32), in_=d_words.bitcast(I32).rearrange("b p n -> p b n")
        )
        for q in range(4):
            nc.sync.dma_start(
                out=d_sc[32 * q : 32 * q + 4, :, :].bitcast(I32),
                in_=d_scales[:, 4 * q : 4 * q + 4, :].bitcast(I32).rearrange("b q n -> q b n"),
            )

        xb, xt, xq, xps = {}, {}, {}, {}

        def interleave_x(i):
            xb[i] = sb([P, 512, 4], BF16, f"xb{i}", bufs=3, tag="pre")
            dst = xb[i][:].rearrange("p (t m) j -> p t m j", t=4)
            src = raw[i // 2][:, i % 2].rearrange("p j (m t) -> p t m j", t=4)
            if XI_ENGINE[i] == "*":
                nc.vector.tensor_copy(out=dst[:, 0:2], in_=src[:, 0:2])
                nc.scalar.copy(out=dst[:, 2], in_=src[:, 2])
                nc.gpsimd.tensor_scalar(
                    out=dst[:, 3],
                    in0=src[:, 3],
                    scalar1=1.0,
                    scalar2=0.0,
                    op0=ALU.mult,
                    op1=ALU.add,
                )
            elif XI_ENGINE[i] == "S":
                nc.scalar.copy(out=dst, in_=src)
            else:
                nc.gpsimd.tensor_scalar(
                    out=dst, in0=src, scalar1=1.0, scalar2=0.0, op0=ALU.mult, op1=ALU.add
                )

        def transpose_x(i):
            words = raw[i // 2][:].rearrange("p s j e -> p (s j e)").bitcast(F32)
            for k in range(2):
                ps = bank([P, 2, 2, P], "tr", f"xps{i}_{k}")
                for jj in range(2):
                    base = ((i % 2) * 4 + 2 * k + jj) * 256
                    for u in range(2):
                        nc.tensor.transpose(
                            ps[:, jj, u, :], words[:, base + u : base + 256 : 2], ident[:]
                        )
                xps[i, k] = ps

        def copy_xt(i):
            xt[i] = sb([P, R, 4], BF16, f"xt{i}", bufs=8, tag="four")
            dst = xt[i][:].rearrange("p r t -> p (r t)").bitcast(F32)
            dst = dst.rearrange("p (r j u) -> p r j u", j=4, u=2)
            for k in range(2):
                nc.scalar.copy(
                    out=dst[:, :, 2 * k : 2 * k + 2, :],
                    in_=xps[i, k][:].rearrange("p j u r -> p r j u"),
                )

        def quantize(src, width, name, tag, bufs):
            codes = sb([P, width], U32, name + "c", bufs=bufs, tag=tag + "c")
            scales = sb([P, width], U8, name + "s", bufs=bufs, tag=tag + "s")
            nc.vector.quantize_mx(out=codes[:].bitcast(FP8X4), scales=scales[:], in_=src)
            return codes, scales

        def quantize_x(i):
            xq[i] = quantize(xb[i][:].rearrange("p c j -> p (c j)"), 512, f"xq{i}", "xq", 8)

        h = []
        for g in range(NB):
            hg = sb([P, 2, 2, S, C, 2], F32, f"h{g}", bufs=5, tag="big")
            h.append(hg)

        hps = {}

        def stage1(i, g):
            ps = bank([P, 4, P], "mx", f"hps{i}_{g}")
            hps[i, g] = ps
            codes, scales = xq[i]
            cols = slice(P * g, P * g + P)
            for t in range(4):
                tc_ = slice(P * t, P * t + P)
                nc.tensor.matmul_mx(
                    out=ps[:, t, :],
                    lhsT=codes[:, tc_].bitcast(FP8X4),
                    lhsT_scale=scales[:, tc_],
                    rhs=a_w[:, 256 * g : 256 * g + 256].bitcast(FP4X4),
                    rhs_scale=af_scales[:, 0, cols],
                    start=True,
                    stop=True,
                )

        def add_h(i, g):
            ps = hps[i, g]
            cols = slice(P * g, P * g + P)
            nc.vector.tensor_tensor(
                out=h[g][:, :, :, i],
                in0=ps[:].rearrange("p (u e) (b c) -> p u b c e", u=2, b=2),
                in1=xt[i][:, cols, :].rearrange("p (b c) (u e) -> p u b c e", u=2, b=2),
                op=ALU.add,
            )

        for i in range(2):
            interleave_x(i)
            transpose_x(i)
            copy_xt(i)
            quantize_x(i)
        interleave_x(2)
        interleave_x(3)
        for i in range(S):
            stage1(i, 0)
            stage1(i, 1)
            if i + 2 < S:
                quantize_x(i + 2)
            add_h(i, 0)
            stage1(i, 2)
            add_h(i, 1)
            stage1(i, 3)
            add_h(i, 2)
            add_h(i, 3)
            if i + 4 < S:
                interleave_x(i + 4)
            if i + 2 < S:
                transpose_x(i + 2)
                copy_xt(i + 2)

        f_p = sb([P, 1024], U8, "f_p")
        nc.gpsimd.tensor_copy(
            out=f_p[:].rearrange("p (t m k) -> p t m k", t=4, k=2),
            in_=f_w[:].rearrange("p (m t k) -> p t m k", t=4, k=2),
        )
        f_sc = sb([P, 512], U8, "f_sc")
        nc.gpsimd.tensor_copy(
            out=f_sc[:].rearrange("p (t m) -> p t m", t=4),
            in_=af_scales[:, 1, :].rearrange("p (m t) -> p t m", t=4),
        )

        trace_f = sb([P, P], F32, "trace_f")
        nc.vector.tensor_copy(out=trace_f[:], in_=trace_rows[:])
        tps = bank([P, P], "tr", "tps")
        nc.tensor.transpose(tps[:], trace_f[:], ident[:])
        trace_c = sb([P, 32], F32, "trace_c")
        nc.scalar.copy(out=trace_c[:], in_=tps[:, 0:32])

        hb, hq, yt, yb, yq, rr, zt = {}, {}, {}, {}, {}, {}, {}
        fps, dps, yps = {}, {}, {}

        def hband(b):
            return h[b // 2][:, :, b % 2]

        def cast(b, half):
            if half == 0:
                hb[b] = sb([P, 2048], BF16, f"hb{b}", bufs=3, tag="pre")
            nc.scalar.copy(
                out=hb[b][:, 1024 * half : 1024 * half + 1024].rearrange("p (n u e) -> p n u e", u=2, e=2),
                in_=hband(b)[:, :, 4 * half : 4 * half + 4].rearrange("p u i c e -> p (i c) u e"),
            )

        def residual(b):
            rr[b] = sb([P, 4, 512], F32, f"rr{b}", bufs=4, tag="wide")
            src = hband(b).rearrange("p u i c e -> p u e (i c)")
            for t in range(4):
                nc.gpsimd.tensor_scalar(
                    out=rr[b][:, t, :],
                    in0=src[:, t // 2, t % 2],
                    scalar1=gain_f[:, t : t + 1],
                    scalar2=0.0,
                    op0=ALU.mult,
                    op1=ALU.add,
                )

        def quantize_h(b):
            hq[b] = quantize(hb[b][:], 512, f"hq{b}", "hq", 3)

        def f_pass(ps, b, t, stop):
            codes, scales = hq[b]
            nc.tensor.matmul_mx(
                out=ps[:],
                lhsT=f_p[:, 256 * t : 256 * t + 256].bitcast(FP4X4),
                lhsT_scale=f_sc[:, P * t : P * t + P],
                rhs=codes[:].bitcast(FP8X4),
                rhs_scale=scales[:],
                start=True,
                stop=stop,
            )

        def stage2(b, ts):
            for t in ts:
                fps[b, t] = bank([P, 512], "mx", f"fps{b}_{t}")
                f_pass(fps[b, t], b, t, True)

        def add_y(b, ts):
            if ts[0] == 0:
                yt[b] = sb([P, 4, 512], BF16, f"yt{b}", bufs=8, tag="four")
            src = hband(b).rearrange("p v i (k u e) w -> p v w u (i k) e", u=2, e=2)
            for t in ts:
                nc.vector.tensor_tensor(
                    out=yt[b][:, t, :].rearrange("p (u x e) -> p u x e", u=2, e=2),
                    in0=fps[b, t][:].rearrange("p (x u e) -> p u x e", u=2, e=2),
                    in1=src[:, t // 2, t % 2],
                    op=ALU.add,
                )

        def transpose_y(b, half):
            words = yt[b][:].rearrange("p t c -> p (t c)").bitcast(F32)
            ps = bank([P, 2, 2, P], "tr", f"yps{b}_{half}")
            for tt in range(2):
                for u in range(2):
                    base = (2 * half + tt) * 256 + u * P
                    nc.tensor.transpose(ps[:, tt, u, :], words[:, base : base + P], ident[:])
            yps[b, half] = ps

        def copy_y(b, half):
            if half == 0:
                yb[b] = sb([P, 2048], BF16, f"yb{b}", bufs=8, tag="four")
            dst = yb[b][:].bitcast(F32).rearrange("p (t m u) -> p t m u", t=4, u=2)
            nc.scalar.copy(
                out=dst[:, 2 * half : 2 * half + 2],
                in_=yps[b, half][:].rearrange("p t u m -> p t m u"),
            )

        def quantize_y(b):
            yq[b] = quantize(yb[b][:], 512, f"yq{b}", "yq", 2)

        def stage3(b, ts):
            for t in ts:
                ps = bank([P, 512], "mx", f"dps{b}_{t}")
                f_pass(ps, b, t, False)
                tc_ = slice(P * t, P * t + P)
                codes, scales = yq[b]
                nc.tensor.matmul_mx(
                    out=ps[:],
                    lhsT=codes[:, tc_].bitcast(FP8X4),
                    lhsT_scale=scales[:, tc_],
                    rhs=d_w[:, b, :].bitcast(FP4X4),
                    rhs_scale=d_sc[:, b, :],
                    start=False,
                    stop=True,
                )
                dps[b, t] = ps

        def add_z(b, ts, sources=(0, S)):
            g = b // 2
            i0, i1 = sources
            if b % 2 == 0 and ts[0] == 0:
                zt[g] = sb([P, 4, S, 2, C], F32, f"zt{g}", bufs=5, tag="big")
            for t in ts:
                nc.vector.scalar_tensor_tensor(
                    out=zt[g][:, t, i0:i1, b % 2, :],
                    in0=dps[b, t][:, C * i0 : C * i1].rearrange("p (i c) -> p i c", c=C),
                    scalar=gain_f[:, t : t + 1],
                    in1=rr[b][:, t, C * i0 : C * i1].rearrange("p (i c) -> p i c", c=C),
                    op0=ALU.mult,
                    op1=ALU.add,
                )

        def finish_z(g, sources, share):
            banks = {}
            for i in sources:
                ps = bank([P, 4, P], "tr", f"zps{g}_{i}")
                for t in range(4):
                    nc.tensor.transpose(
                        ps[:, t, :], zt[g][:, t, i].rearrange("p b c -> p (b c)"), ident[:]
                    )
                banks[i] = ps
            for i in sources:
                o = sb([P, T], F32, f"o{g}_{i}", bufs=6, tag="o")
                dst = o[:].rearrange("p (m t) -> p m t", t=4)
                src = banks[i][:].rearrange("p t m -> p m t")
                tr = trace_c[:, 4 * i + g : 4 * i + g + 1]
                if share and i % 2 == 1:
                    nc.vector.tensor_scalar_mul(out=dst, in0=src, scalar1=tr)
                else:
                    nc.scalar.activation(out=dst, in_=src, func=ACT.Copy, scale=tr)
                nc.sync.dma_start(out=out[i, P * g : P * g + P, :], in_=o[:])

        FIRST, SECOND = (0, 1), (2, 3)

        def finish_step(k, part):
            if k >= 2:
                first = 4 * (k % 2)
                part((k - 2) // 2, range(first, first + 4), k >= B)

        for b in (0, 1):
            cast(b, 0)
            cast(b, 1)
        residual(0)
        residual(1)
        quantize_h(0)
        stage2(0, FIRST)
        stage2(0, SECOND)
        for k in range(B + 2):
            if k < B:
                add_y(k, FIRST)
            if 1 <= k <= B:
                stage3(k - 1, FIRST)
            if k < B:
                add_y(k, SECOND)
                transpose_y(k, 0)
                transpose_y(k, 1)
                copy_y(k, 0)
                copy_y(k, 1)
            if 1 <= k <= B:
                add_z(k - 1, FIRST, (0, S if k < B else 4))
                stage3(k - 1, SECOND)
            if k + 1 < B:
                quantize_h(k + 1)
                stage2(k + 1, FIRST)
            if k + 2 < B:
                cast(k + 2, 0)
            if k + 1 < B:
                stage2(k + 1, SECOND)
            if 1 <= k <= B:
                add_z(k - 1, SECOND, (0, S if k < B else 4))
            if k == B:
                add_z(k - 1, FIRST, (4, S))
                add_z(k - 1, SECOND, (4, S))
            if k < B:
                quantize_y(k)
            if k + 2 < B:
                residual(k + 2)
            finish_step(k, finish_z)
            if k + 2 < B:
                cast(k + 2, 1)
